import numpy as np
import ml_dtypes


def mxq(x, axis, fmt="e4m3"):
    dtype, down = {"e4m3": (ml_dtypes.float8_e4m3fn, 7), "e5m2": (ml_dtypes.float8_e5m2, 14)}[fmt]
    v = np.moveaxis(np.asarray(x, np.float32).astype(ml_dtypes.bfloat16).astype(np.float64), axis, -1)
    blocks = v.reshape(v.shape[:-1] + (-1, 32))
    amax = np.abs(blocks).max(-1, keepdims=True)
    byte = np.maximum(np.where(amax > 0, np.frexp(amax)[1] - 1 + 127, 0) - down, 1)
    scale = np.exp2(byte - 127.0)
    codes = (blocks / scale).astype(np.float32).astype(dtype).astype(np.float64)
    return np.moveaxis((codes * scale).reshape(v.shape), -1, axis)


WIDE = False


def mx_kscale(k):
    if not WIDE:
        return np.ones(k)
    levels = np.array([10, -10, 5, -5, 0])
    if k % 512:
        return np.exp2(np.random.permutation(np.resize(levels, k // 32))).repeat(32)
    a = np.empty((k // 512, 16))
    for p in range(k // 512):
        a[p, :8] = np.random.permutation(np.resize(levels, 8))
        for g in range(8):
            far = levels[np.abs(levels - a[p, g]) >= 10]
            a[p, g + 8] = far[np.random.randint(len(far))]
    return np.exp2(a.ravel()).repeat(32)


def f64(x):
    return np.asarray(x).astype(np.float64)


def striped(idx):
    return np.tile(np.asarray(idx).reshape(-1, 16).T, (8, 1)).astype(np.uint16)


def unstriped(offs):
    return offs[:16].T.reshape(-1).astype(np.int64)


E2M1 = np.array([0.0, 0.5, 1.0, 1.5, 2.0, 3.0, 4.0, 6.0, -0.0, -0.5, -1.0, -1.5, -2.0, -3.0, -4.0, -6.0])


def pack_weight(w, fmt):
    k, n = w.shape
    w = f64(np.asarray(w, np.float32).astype(ml_dtypes.bfloat16)).reshape(k // 32, 32, n)
    amax = np.abs(w).max(1)
    if fmt == "e4m3":
        byte = np.frexp(amax)[1] - 1 + 127 - 7
    else:
        mant, ex = np.frexp(amax / 6.0)
        byte = np.where(mant > 0.5, ex, ex - 1) + 127
    byte = np.clip(np.where(amax > 0, byte, 1), 1, 254)
    scaled = (w * np.exp2(127.0 - byte)[:, None, :]).reshape(k, n).astype(np.float32)
    by_word = np.ascontiguousarray(scaled.reshape(k // 512, 128, 4, n).transpose(0, 1, 3, 2))
    if fmt == "e4m3":
        words = by_word.astype(ml_dtypes.float8_e4m3fn).view(np.uint8)
    else:
        c = by_word.astype(ml_dtypes.float4_e2m1fn).view(np.uint8) & 0xF
        words = (c[..., 0::2] | (c[..., 1::2] << 4)).reshape(k // 512, 128, 2 * n)
    return np.ascontiguousarray(words), np.ascontiguousarray(byte.astype(np.uint8).reshape(k // 512, 16, n))


def unpack_weight(words, scales, fmt):
    g, _, n = scales.shape
    words = np.ascontiguousarray(words).reshape(g, 128, n, -1)
    if fmt == "e4m3":
        vals = words.view(ml_dtypes.float8_e4m3fn).astype(np.float64)
    else:
        nib = np.empty((g, 128, n, 4), np.uint8)
        nib[..., 0::2] = words & 0xF
        nib[..., 1::2] = words >> 4
        vals = E2M1[nib]
    vals = vals * np.repeat(np.exp2(scales.astype(np.float64) - 127.0), 8, axis=1)[..., None]
    return vals.transpose(0, 1, 3, 2).reshape(g * 512, n)


D, E, T, I, Q = 512, 512, 2048, 512, 128


def setup_inputs():
    n = np.random.standard_normal
    idx = np.random.permutation(T)[:I]
    fd = mx_kscale(D)
    fe = mx_kscale(E)
    keysp = pack_weight(n((D, T)) / fd[:, None], "e2m1")
    valsp = pack_weight(n((E, T)) / fe[:, None], "e2m1")
    return {
        "query": (n((D, Q)) * 0.6 / np.sqrt(D) * fd[:, None]).astype(np.float32),
        "keys_words": keysp[0],
        "keys_scales": keysp[1],
        "lprior": np.tile(np.random.uniform(-7.5, -5.0, T), (128, 1)).astype(np.float32),
        "strict": (np.random.uniform(0.2, 0.8, (Q, 1))).astype(np.float32),
        "gout": (n((E, Q)) * 1 / np.sqrt(E) * fe[:, None]).astype(np.float32),
        "vals_words": valsp[0],
        "vals_scales": valsp[1],
        "base": (0.5 * n((Q, T))).astype(np.float32),
        "gq1": (np.random.uniform(0.3, 1.5, (Q, 1))).astype(np.float32),
        "offs": striped(idx),
    }


def reference(query, keys_words, keys_scales, lprior, strict, gout, vals_words, vals_scales, base, gq1, offs):
    idx = unstriped(offs)
    keysu = unpack_weight(keys_words, keys_scales, "e2m1")
    valsu = unpack_weight(vals_words, vals_scales, "e2m1")
    queryq = mxq(f64(query), 0, "e4m3")
    keysidxg = keysu[:, idx]
    a = queryq.T @ keysidxg
    b = a - np.max(a, axis=1, keepdims=True)
    p = np.exp(b)
    z = np.sum(p, axis=1, keepdims=True)
    goutq = mxq(f64(gout), 0, "e4m3")
    valsidxg = valsu[:, idx]
    c0 = goutq.T @ valsidxg
    dz = f64(strict) / z - np.sum(p * c0, axis=1, keepdims=True) / np.square(z) - f64(strict) * (-1.0) * np.sum(p * (b - f64(lprior)[:1][:, idx]), axis=1, keepdims=True) / np.square(z)
    dp = 1.0 / z * c0 + f64(strict) * (-1.0) / z * (b - f64(lprior)[:1][:, idx]) + dz
    db = f64(strict) * (-1.0) / z * p + dp * p
    hdb = db * 512.0 * 2.0 * 512.0
    hdp = hdb * p
    hdz = np.sum(hdp, axis=1, keepdims=True)
    hz = hdz * (-1.0) * np.sum(p * c0, axis=1, keepdims=True) / np.square(np.square(z)) * (-1.0) * z * 2.0 + hdz * (-1.0) * f64(strict) * (-1.0) * np.sum(p * (b - f64(lprior)[:1][:, idx]), axis=1, keepdims=True) / np.square(np.square(z)) * (-1.0) * z * 2.0 - np.sum(hdb * p, axis=1, keepdims=True) * f64(strict) * (-1.0) / np.square(z) - np.sum(hdp * c0, axis=1, keepdims=True) / np.square(z) - np.sum(hdp * (b - f64(lprior)[:1][:, idx]), axis=1, keepdims=True) * f64(strict) * (-1.0) / np.square(z) - hdz * f64(strict) / np.square(z)
    hp = hdb * f64(strict) * (-1.0) / z + hdb * dp + hdz * (-1.0) / np.square(z) * c0 + hdz * (-1.0) / np.square(z) * f64(strict) * (-1.0) * (b - f64(lprior)[:1][:, idx]) + hz
    hb = hdp * f64(strict) * (-1.0) / z + hdz * (-1.0) / np.square(z) * f64(strict) * (-1.0) * p + hp * p
    gs = hb * f64(gq1)
    gf = np.zeros((Q, T))
    gf[:, idx] = gs
    y = f64(base) + gf
    return y

@@ -1,0 +1,179 @@
+from contextlib import ExitStack
+
+import concourse.mybir as mybir
+
+D, E, T, I, Q = 512, 512, 2048, 512, 128
+FLOPS = 2 * Q * I * (D + E)
+
+F32 = mybir.dt.float32
+BF16 = mybir.dt.bfloat16
+I32 = mybir.dt.int32
+U32 = mybir.dt.uint32
+U16 = mybir.dt.uint16
+U8 = mybir.dt.uint8
+FP8X4 = mybir.dt.float8_e4m3fn_x4
+FP4X4 = mybir.dt.float4_e2m1fn_x4
+ALU = mybir.AluOpType
+ACT = mybir.ActivationFunctionType
+
+P = 128
+PACK = 4
+PENALTY = 512.0 * 2.0 * 512.0
+EARLY_SLOTS = 384
+STORE_WIDTHS = (256, 512, 512, 512, 256)
+
+
+def tile_attend_gppriorpull_kernel(tc, query, keys_words, keys_scales, lprior, strict, gout,
+                                    vals_words, vals_scales, base, gq1, offs, out):
+    nc = tc.nc
+    with ExitStack() as ctx:
+        sb = ctx.enter_context(tc.tile_pool(name="sb", bufs=1))
+        ps = ctx.enter_context(tc.psum_pool(name="ps", bufs=1))
+
+        def tile(name, width, dtype, tag=None):
+            return sb.tile([P, width], dtype, name=name, tag=tag or name, align_bytes=64)
+
+        offsets = sb.tile([P, I // 16], U16, name="offsets")
+        key_words = tile("key_words", T, U16)
+        key_bytes = tile("key_bytes", T, U8)
+        val_words = tile("val_words", T, U16)
+        val_bytes = tile("val_bytes", T, U8)
+        query_raw = tile("query_raw", PACK * Q, F32)
+        gout_raw = tile("gout_raw", PACK * Q, F32)
+        s = tile("s", 1, F32)
+        row_factor = tile("row_factor", 1, F32)
+
+        def load_scale_rows(plane, rows):
+            for quad in range(4):
+                nc.sync.dma_start(out=plane[32 * quad:32 * quad + 4, :].bitcast(I32),
+                                  in_=rows[0, 4 * quad:4 * quad + 4, :].bitcast(I32))
+
+        def load_rows(raw, src):
+            nc.sync.dma_start(out=raw[:], in_=src.rearrange("(p j) q -> p (j q)", j=PACK))
+
+        nc.vector.memset(key_bytes[:].bitcast(I32), 0)
+        nc.vector.memset(val_bytes[:].bitcast(I32), 0)
+
+        warm = tile("warm", 1, F32)
+        warm_out = tile("warm_out", 1, F32)
+        nc.gpsimd.memset(warm[:], 0.0)
+        nc.scalar.activation(warm_out[:], warm[:], ACT.Exp)
+
+        nc.sync.dma_start(offsets[:], offs)
+        nc.sync.dma_start(out=key_words[:].bitcast(I32), in_=keys_words[0].bitcast(I32))
+        nc.sync.dma_start(out=val_words[:].bitcast(I32), in_=vals_words[0].bitcast(I32))
+        load_scale_rows(key_bytes, keys_scales)
+        load_rows(query_raw, query)
+        load_rows(gout_raw, gout)
+        load_scale_rows(val_bytes, vals_scales)
+        nc.gpsimd.dma_start(out=s[:], in_=strict)
+        nc.gpsimd.dma_start(out=row_factor[:], in_=gq1)
+
+        def round_and_interleave(name, raw):
+            grouped = tile(name, PACK * Q, BF16)
+            nc.scalar.copy(out=grouped[:].rearrange("p (q j) -> p q j", j=PACK),
+                           in_=raw[:].rearrange("p (j q) -> p q j", j=PACK))
+            return grouped
+
+        def quantise(name, grouped):
+            codes = tile(name + "_codes", Q, U32)
+            scales = tile(name + "_scales", Q, U8)
+            nc.vector.quantize_mx(out=codes[:].bitcast(FP8X4), scales=scales[:], in_=grouped[:])
+            return codes, scales
+
+        def gather(name, window, dtype):
+            picked = tile(name, I, dtype)
+            nc.vector.tensor_copy(picked[:], window[:].indirect(offsets[:]))
+            return picked
+
+        def product(name, rows, words, scale_bytes):
+            acc = ps.tile([P, I], F32, name=name)
+            nc.tensor.matmul_mx(out=acc[:], lhsT=rows[0][:].bitcast(FP8X4), lhsT_scale=rows[1][:],
+                                rhs=words[:].bitcast(FP4X4), rhs_scale=scale_bytes[:], start=True, stop=True)
+            return acc
+
+        query_bf = round_and_interleave("query_bf", query_raw)
+        gout_bf = round_and_interleave("gout_bf", gout_raw)
+
+        picked_key_words = gather("picked_key_words", key_words, U16)
+        prior = tile("prior", T, F32, tag="key_words")
+        nc.sync.dma_start(out=prior[:], in_=lprior)
+        picked_val_words = gather("picked_val_words", val_words, U16)
+        result = tile("result", T, F32, tag="val_words")
+        nc.sync.dma_start(out=result[:], in_=base)
+        picked_key_bytes = gather("picked_key_bytes", key_bytes, U8)
+        query_mx = quantise("query", query_bf)
+        a = product("a", query_mx, picked_key_words, picked_key_bytes)
+        gout_mx = quantise("gout", gout_bf)
+        placed = tile("placed", T, F32, tag="gout_bf")
+        nc.gpsimd.memset(placed[:], 0.0)
+        picked_val_bytes = gather("picked_val_bytes", val_bytes, U8)
+        c0 = product("c0", gout_mx, picked_val_words, picked_val_bytes)
+
+        neg_a = tile("neg_a", I, F32, tag="val_bytes")
+        neg_max = tile("neg_max", 1, F32)
+        nc.vector.tensor_scalar(out=neg_a[:], in0=a[:], scalar1=-1.0, scalar2=None, op0=ALU.mult, op1=ALU.min,
+                                accum_out=neg_max[:])
+        p = tile("p", I, F32)
+        z = tile("z", 1, F32)
+        nc.scalar.activation(p[:], neg_a[:], ACT.Exp, bias=neg_max[:], scale=-1.0, accum_out=z[:])
+
+        early, late = slice(0, EARLY_SLOTS), slice(EARLY_SLOTS, I)
+
+        def prior_minus_score(name, slots, tag=None):
+            gap = tile(name, slots.stop - slots.start, F32, tag=tag)
+            listed = offsets[:, slots.start // 16:slots.stop // 16]
+            nc.vector.tensor_tensor(gap[:], prior[:].indirect(listed), neg_a[:, slots], ALU.add)
+            return gap
+
+        gap_early = prior_minus_score("gap_early", early)
+        inv_z = tile("inv_z", 1, F32)
+        nc.vector.reciprocal(inv_z[:], z[:])
+        gap_late = prior_minus_score("gap_late", late, tag="z")
+        gain = tile("gain", 1, F32)
+        neg_gain = tile("neg_gain", 1, F32)
+        nc.scalar.activation(gain[:], row_factor[:], ACT.Copy, scale=PENALTY)
+        nc.scalar.activation(neg_gain[:], row_factor[:], ACT.Copy, scale=-PENALTY)
+        w = tile("w", I, F32)
+        w_sq = tile("w_sq", I, F32)
+        w_gain = tile("w_gain", I, F32)
+        w_neg_gain = tile("w_neg_gain", I, F32)
+        nc.scalar.activation(w[:], p[:], ACT.Copy, scale=inv_z[:])
+        nc.scalar.activation(w_sq[:], p[:], ACT.Square, scale=inv_z[:])
+        nc.scalar.activation(w_gain[:], w[:], ACT.Copy, scale=gain[:])
+        nc.scalar.activation(w_neg_gain[:], w[:], ACT.Copy, scale=neg_gain[:])
+
+        u = tile("u", I, F32)
+        for slots, gap in ((early, gap_early), (late, gap_late)):
+            nc.vector.scalar_tensor_tensor(u[:, slots], gap[:], s[:], c0[:, slots], ALU.mult, ALU.add)
+        wu = tile("wu", I, F32)
+        u_mean = tile("u_mean", 1, F32)
+        nc.vector.scalar_tensor_tensor(wu[:], u[:], inv_z[:], p[:], ALU.mult, ALU.mult, accum_out=u_mean[:])
+        u_mean_s = tile("u_mean_s", 1, F32)
+        nc.scalar.activation(u_mean_s[:], u_mean[:], ACT.Identity, bias=s[:])
+        d = tile("d", I, F32)
+        nc.vector.scalar_tensor_tensor(d[:], u[:], u_mean[:], w[:], ALU.subtract, ALU.mult)
+        wd = tile("wd", I, F32)
+        sum_wd = tile("sum_wd", 1, F32)
+        nc.vector.scalar_tensor_tensor(wd[:], u[:], u_mean[:], w_sq[:], ALU.subtract, ALU.mult, accum_out=sum_wd[:])
+        dd = tile("dd", I, F32)
+        sum_dd = tile("sum_dd", 1, F32)
+        nc.scalar.activation(dd[:], d[:], ACT.Square, accum_out=sum_dd[:])
+        second = tile("second", I, F32)
+        nc.scalar.activation(second[:], w_neg_gain[:], ACT.Copy, scale=sum_dd[:])
+        y = tile("y", I, F32)
+        first = tile("first", I, F32)
+        halves = (slice(0, I // 2), slice(I // 2, I))
+        for h in halves:
+            nc.vector.scalar_tensor_tensor(y[:, h], u[:, h], u_mean_s[:], w_gain[:, h], ALU.subtract, ALU.mult)
+        for h in halves:
+            nc.vector.scalar_tensor_tensor(first[:, h], d[:, h], sum_wd[:], y[:, h], ALU.subtract, ALU.mult)
+
+        nc.vector.tensor_tensor(placed[:].indirect(offsets[:]), first[:], second[:], ALU.add)
+
+        start = 0
+        for width in STORE_WIDTHS:
+            cols = slice(start, start + width)
+            nc.vector.tensor_tensor(result[:, cols], result[:, cols], placed[:, cols], ALU.add)
+            nc.sync.dma_start(out=out[:, cols], in_=result[:, cols])
+            start += width

@@ -19,7 +19,6 @@ ACT = mybir.ActivationFunctionType
 P = 128
 PACK = 4
 PENALTY = 512.0 * 2.0 * 512.0
-EARLY_SLOTS = 384
 STORE_WIDTHS = (256, 512, 512, 512, 256)
 
 
@@ -40,6 +39,9 @@ def tile_attend_gppriorpull_kernel(tc, query, keys_words, keys_scales, lprior, s
         val_bytes = tile("val_bytes", T, U8)
         query_raw = tile("query_raw", PACK * Q, F32)
         gout_raw = tile("gout_raw", PACK * Q, F32)
+        prior = tile("prior", T, F32)
+        result = tile("result", T, F32)
+        placed = tile("placed", T, F32)
         s = tile("s", 1, F32)
         row_factor = tile("row_factor", 1, F32)
 
@@ -53,26 +55,24 @@ def tile_attend_gppriorpull_kernel(tc, query, keys_words, keys_scales, lprior, s
 
         nc.vector.memset(key_bytes[:].bitcast(I32), 0)
         nc.vector.memset(val_bytes[:].bitcast(I32), 0)
-
-        warm = tile("warm", 1, F32)
-        warm_out = tile("warm_out", 1, F32)
-        nc.gpsimd.memset(warm[:], 0.0)
-        nc.scalar.activation(warm_out[:], warm[:], ACT.Exp)
+        nc.vector.memset(placed[:], 0.0)
 
         nc.sync.dma_start(offsets[:], offs)
         nc.sync.dma_start(out=key_words[:].bitcast(I32), in_=keys_words[0].bitcast(I32))
-        nc.sync.dma_start(out=val_words[:].bitcast(I32), in_=vals_words[0].bitcast(I32))
         load_scale_rows(key_bytes, keys_scales)
         load_rows(query_raw, query)
+        nc.sync.dma_start(out=val_words[:].bitcast(I32), in_=vals_words[0].bitcast(I32))
         load_rows(gout_raw, gout)
         load_scale_rows(val_bytes, vals_scales)
-        nc.gpsimd.dma_start(out=s[:], in_=strict)
-        nc.gpsimd.dma_start(out=row_factor[:], in_=gq1)
+        nc.sync.dma_start(out=prior[:], in_=lprior)
+        nc.sync.dma_start(out=s[:], in_=strict)
+        nc.sync.dma_start(out=row_factor[:], in_=gq1)
+        nc.sync.dma_start(out=result[:], in_=base)
 
         def round_and_interleave(name, raw):
             grouped = tile(name, PACK * Q, BF16)
-            nc.scalar.copy(out=grouped[:].rearrange("p (q j) -> p q j", j=PACK),
-                           in_=raw[:].rearrange("p (j q) -> p q j", j=PACK))
+            nc.scalar.activation(grouped[:].rearrange("p (q j) -> p q j", j=PACK),
+                                 raw[:].rearrange("p (j q) -> p q j", j=PACK), ACT.Copy)
             return grouped
 
         def quantise(name, grouped):
@@ -81,8 +81,8 @@ def tile_attend_gppriorpull_kernel(tc, query, keys_words, keys_scales, lprior, s
             nc.vector.quantize_mx(out=codes[:].bitcast(FP8X4), scales=scales[:], in_=grouped[:])
             return codes, scales
 
-        def gather(name, window, dtype):
-            picked = tile(name, I, dtype)
+        def gather(name, window, dtype, tag=None):
+            picked = tile(name, I, dtype, tag=tag)
             nc.vector.tensor_copy(picked[:], window[:].indirect(offsets[:]))
             return picked
 
@@ -96,21 +96,12 @@ def tile_attend_gppriorpull_kernel(tc, query, keys_words, keys_scales, lprior, s
         gout_bf = round_and_interleave("gout_bf", gout_raw)
 
         picked_key_words = gather("picked_key_words", key_words, U16)
-        prior = tile("prior", T, F32, tag="key_words")
-        nc.sync.dma_start(out=prior[:], in_=lprior)
-        picked_val_words = gather("picked_val_words", val_words, U16)
-        result = tile("result", T, F32, tag="val_words")
-        nc.sync.dma_start(out=result[:], in_=base)
         picked_key_bytes = gather("picked_key_bytes", key_bytes, U8)
         query_mx = quantise("query", query_bf)
         a = product("a", query_mx, picked_key_words, picked_key_bytes)
-        gout_mx = quantise("gout", gout_bf)
-        placed = tile("placed", T, F32, tag="gout_bf")
-        nc.gpsimd.memset(placed[:], 0.0)
-        picked_val_bytes = gather("picked_val_bytes", val_bytes, U8)
-        c0 = product("c0", gout_mx, picked_val_words, picked_val_bytes)
+        picked_val_words = gather("picked_val_words", val_words, U16, tag="query_bf")
 
-        neg_a = tile("neg_a", I, F32, tag="val_bytes")
+        neg_a = tile("neg_a", I, F32, tag="val_words")
         neg_max = tile("neg_max", 1, F32)
         nc.vector.tensor_scalar(out=neg_a[:], in0=a[:], scalar1=-1.0, scalar2=None, op0=ALU.mult, op1=ALU.min,
                                 accum_out=neg_max[:])
@@ -118,18 +109,19 @@ def tile_attend_gppriorpull_kernel(tc, query, keys_words, keys_scales, lprior, s
         z = tile("z", 1, F32)
         nc.scalar.activation(p[:], neg_a[:], ACT.Exp, bias=neg_max[:], scale=-1.0, accum_out=z[:])
 
-        early, late = slice(0, EARLY_SLOTS), slice(EARLY_SLOTS, I)
+        gout_mx = quantise("gout", gout_bf)
+        picked_val_bytes = gather("picked_val_bytes", val_bytes, U8)
+        c0 = product("c0", gout_mx, picked_val_words, picked_val_bytes)
 
-        def prior_minus_score(name, slots, tag=None):
-            gap = tile(name, slots.stop - slots.start, F32, tag=tag)
-            listed = offsets[:, slots.start // 16:slots.stop // 16]
-            nc.vector.tensor_tensor(gap[:], prior[:].indirect(listed), neg_a[:, slots], ALU.add)
-            return gap
-
-        gap_early = prior_minus_score("gap_early", early)
-        inv_z = tile("inv_z", 1, F32)
+        inv_z = tile("inv_z", 1, F32, tag="val_bytes")
         nc.vector.reciprocal(inv_z[:], z[:])
-        gap_late = prior_minus_score("gap_late", late, tag="z")
+
+        halves = (slice(0, I // 2), slice(I // 2, I))
+        gap = tile("gap", I, F32, tag="gout_bf")
+        for h in halves:
+            listed = offsets[:, h.start // 16:h.stop // 16]
+            nc.vector.tensor_tensor(gap[:, h], prior[:].indirect(listed), neg_a[:, h], ALU.add)
+
         gain = tile("gain", 1, F32)
         neg_gain = tile("neg_gain", 1, F32)
         nc.scalar.activation(gain[:], row_factor[:], ACT.Copy, scale=PENALTY)
@@ -144,8 +136,8 @@ def tile_attend_gppriorpull_kernel(tc, query, keys_words, keys_scales, lprior, s
         nc.scalar.activation(w_neg_gain[:], w[:], ACT.Copy, scale=neg_gain[:])
 
         u = tile("u", I, F32)
-        for slots, gap in ((early, gap_early), (late, gap_late)):
-            nc.vector.scalar_tensor_tensor(u[:, slots], gap[:], s[:], c0[:, slots], ALU.mult, ALU.add)
+        for h in halves:
+            nc.vector.scalar_tensor_tensor(u[:, h], gap[:, h], s[:], c0[:, h], ALU.mult, ALU.add)
         wu = tile("wu", I, F32)
         u_mean = tile("u_mean", 1, F32)
         nc.vector.scalar_tensor_tensor(wu[:], u[:], inv_z[:], p[:], ALU.mult, ALU.mult, accum_out=u_mean[:])
@@ -163,7 +155,6 @@ def tile_attend_gppriorpull_kernel(tc, query, keys_words, keys_scales, lprior, s
         nc.scalar.activation(second[:], w_neg_gain[:], ACT.Copy, scale=sum_dd[:])
         y = tile("y", I, F32)
         first = tile("first", I, F32)
-        halves = (slice(0, I // 2), slice(I // 2, I))
         for h in halves:
             nc.vector.scalar_tensor_tensor(y[:, h], u[:, h], u_mean_s[:], w_gain[:, h], ALU.subtract, ALU.mult)
         for h in halves:

@@ -18,8 +18,11 @@ ACT = mybir.ActivationFunctionType
 
 P = 128
 PACK = 4
+QUADRANT = 32
+SCALE_ROWS = 4
+LIST_ROWS = 16
 PENALTY = 512.0 * 2.0 * 512.0
-STORE_WIDTHS = (256, 512, 512, 512, 256)
+STORE_WIDTHS = (128, 384, 512, 512, 384, 128)
 
 
 def tile_attend_gppriorpull_kernel(tc, query, keys_words, keys_scales, lprior, strict, gout,
@@ -29,10 +32,10 @@ def tile_attend_gppriorpull_kernel(tc, query, keys_words, keys_scales, lprior, s
         sb = ctx.enter_context(tc.tile_pool(name="sb", bufs=1))
         ps = ctx.enter_context(tc.psum_pool(name="ps", bufs=1))
 
-        def tile(name, width, dtype, tag=None):
-            return sb.tile([P, width], dtype, name=name, tag=tag or name, align_bytes=64)
+        def tile(name, width, dtype, reuse=None):
+            return sb.tile([P, width], dtype, name=name, tag=reuse or name, align_bytes=64)
 
-        offsets = sb.tile([P, I // 16], U16, name="offsets")
+        offsets = sb.tile([P, I // LIST_ROWS], U16, name="offsets")
         key_words = tile("key_words", T, U16)
         key_bytes = tile("key_bytes", T, U8)
         val_words = tile("val_words", T, U16)
@@ -45,13 +48,14 @@ def tile_attend_gppriorpull_kernel(tc, query, keys_words, keys_scales, lprior, s
         s = tile("s", 1, F32)
         row_factor = tile("row_factor", 1, F32)
 
-        def load_scale_rows(plane, rows):
-            for quad in range(4):
-                nc.sync.dma_start(out=plane[32 * quad:32 * quad + 4, :].bitcast(I32),
-                                  in_=rows[0, 4 * quad:4 * quad + 4, :].bitcast(I32))
+        def load_scale_rows(scale_tile, rows):
+            for n in range(P // QUADRANT):
+                nc.sync.dma_start(
+                    out=scale_tile[QUADRANT * n:QUADRANT * n + SCALE_ROWS, :].bitcast(I32),
+                    in_=rows[0, SCALE_ROWS * n:SCALE_ROWS * (n + 1), :].bitcast(I32))
 
         def load_rows(raw, src):
-            nc.sync.dma_start(out=raw[:], in_=src.rearrange("(p j) q -> p (j q)", j=PACK))
+            nc.sync.dma_start(out=raw[:], in_=src.rearrange("(p t) q -> p (t q)", t=PACK))
 
         nc.vector.memset(key_bytes[:].bitcast(I32), 0)
         nc.vector.memset(val_bytes[:].bitcast(I32), 0)
@@ -64,15 +68,15 @@ def tile_attend_gppriorpull_kernel(tc, query, keys_words, keys_scales, lprior, s
         nc.sync.dma_start(out=val_words[:].bitcast(I32), in_=vals_words[0].bitcast(I32))
         load_rows(gout_raw, gout)
         load_scale_rows(val_bytes, vals_scales)
+        nc.sync.dma_start(out=row_factor[:], in_=gq1)
         nc.sync.dma_start(out=prior[:], in_=lprior)
         nc.sync.dma_start(out=s[:], in_=strict)
-        nc.sync.dma_start(out=row_factor[:], in_=gq1)
         nc.sync.dma_start(out=result[:], in_=base)
 
         def round_and_interleave(name, raw):
             grouped = tile(name, PACK * Q, BF16)
-            nc.scalar.activation(grouped[:].rearrange("p (q j) -> p q j", j=PACK),
-                                 raw[:].rearrange("p (j q) -> p q j", j=PACK), ACT.Copy)
+            nc.scalar.activation(grouped[:].rearrange("p (q t) -> p q t", t=PACK),
+                                 raw[:].rearrange("p (t q) -> p q t", t=PACK), ACT.Copy)
             return grouped
 
         def quantise(name, grouped):
@@ -81,14 +85,15 @@ def tile_attend_gppriorpull_kernel(tc, query, keys_words, keys_scales, lprior, s
             nc.vector.quantize_mx(out=codes[:].bitcast(FP8X4), scales=scales[:], in_=grouped[:])
             return codes, scales
 
-        def gather(name, window, dtype, tag=None):
-            picked = tile(name, I, dtype, tag=tag)
+        def gather(name, window, dtype, reuse=None):
+            picked = tile(name, I, dtype, reuse=reuse)
             nc.vector.tensor_copy(picked[:], window[:].indirect(offsets[:]))
             return picked
 
-        def product(name, rows, words, scale_bytes):
+        def product(name, rows_mx, words, scale_bytes):
+            codes, scales = rows_mx
             acc = ps.tile([P, I], F32, name=name)
-            nc.tensor.matmul_mx(out=acc[:], lhsT=rows[0][:].bitcast(FP8X4), lhsT_scale=rows[1][:],
+            nc.tensor.matmul_mx(out=acc[:], lhsT=codes[:].bitcast(FP8X4), lhsT_scale=scales[:],
                                 rhs=words[:].bitcast(FP4X4), rhs_scale=scale_bytes[:], start=True, stop=True)
             return acc
 
@@ -99,9 +104,9 @@ def tile_attend_gppriorpull_kernel(tc, query, keys_words, keys_scales, lprior, s
         picked_key_bytes = gather("picked_key_bytes", key_bytes, U8)
         query_mx = quantise("query", query_bf)
         a = product("a", query_mx, picked_key_words, picked_key_bytes)
-        picked_val_words = gather("picked_val_words", val_words, U16, tag="query_bf")
+        picked_val_words = gather("picked_val_words", val_words, U16, reuse="query_raw")
 
-        neg_a = tile("neg_a", I, F32, tag="val_words")
+        neg_a = tile("neg_a", I, F32)
         neg_max = tile("neg_max", 1, F32)
         nc.vector.tensor_scalar(out=neg_a[:], in0=a[:], scalar1=-1.0, scalar2=None, op0=ALU.mult, op1=ALU.min,
                                 accum_out=neg_max[:])
@@ -113,19 +118,19 @@ def tile_attend_gppriorpull_kernel(tc, query, keys_words, keys_scales, lprior, s
         picked_val_bytes = gather("picked_val_bytes", val_bytes, U8)
         c0 = product("c0", gout_mx, picked_val_words, picked_val_bytes)
 
-        inv_z = tile("inv_z", 1, F32, tag="val_bytes")
-        nc.vector.reciprocal(inv_z[:], z[:])
-
-        halves = (slice(0, I // 2), slice(I // 2, I))
-        gap = tile("gap", I, F32, tag="gout_bf")
-        for h in halves:
-            listed = offsets[:, h.start // 16:h.stop // 16]
-            nc.vector.tensor_tensor(gap[:, h], prior[:].indirect(listed), neg_a[:, h], ALU.add)
-
         gain = tile("gain", 1, F32)
         neg_gain = tile("neg_gain", 1, F32)
         nc.scalar.activation(gain[:], row_factor[:], ACT.Copy, scale=PENALTY)
         nc.scalar.activation(neg_gain[:], row_factor[:], ACT.Copy, scale=-PENALTY)
+        inv_z = tile("inv_z", 1, F32, reuse="row_factor")
+        nc.vector.reciprocal(inv_z[:], z[:])
+
+        halves = (slice(0, I // 2), slice(I // 2, I))
+        gap = tile("gap", I, F32, reuse="gout_bf")
+        for h in halves:
+            listed = offsets[:, h.start // LIST_ROWS:h.stop // LIST_ROWS]
+            nc.vector.tensor_tensor(gap[:, h], prior[:].indirect(listed), neg_a[:, h], ALU.add)
+
         w = tile("w", I, F32)
         w_sq = tile("w_sq", I, F32)
         w_gain = tile("w_gain", I, F32)

from contextlib import ExitStack

import concourse.mybir as mybir

D, E, T, I, Q = 512, 512, 2048, 512, 128
FLOPS = 2 * Q * I * (D + E)

F32 = mybir.dt.float32
BF16 = mybir.dt.bfloat16
I32 = mybir.dt.int32
U32 = mybir.dt.uint32
U16 = mybir.dt.uint16
U8 = mybir.dt.uint8
FP8X4 = mybir.dt.float8_e4m3fn_x4
FP4X4 = mybir.dt.float4_e2m1fn_x4
ALU = mybir.AluOpType
ACT = mybir.ActivationFunctionType

P = 128
PACK = 4
QUADRANT = 32
SCALE_ROWS = 4
LIST_ROWS = 16
PENALTY = 512.0 * 2.0 * 512.0
STORE_WIDTHS = (128, 384, 512, 512, 384, 128)


def tile_attend_gppriorpull_kernel(tc, query, keys_words, keys_scales, lprior, strict, gout,
                                    vals_words, vals_scales, base, gq1, offs, out):
    nc = tc.nc
    with ExitStack() as ctx:
        sb = ctx.enter_context(tc.tile_pool(name="sb", bufs=1))
        ps = ctx.enter_context(tc.psum_pool(name="ps", bufs=1))

        def tile(name, width, dtype, reuse=None):
            return sb.tile([P, width], dtype, name=name, tag=reuse or name, align_bytes=64)

        offsets = sb.tile([P, I // LIST_ROWS], U16, name="offsets")
        key_words = tile("key_words", T, U16)
        key_bytes = tile("key_bytes", T, U8)
        val_words = tile("val_words", T, U16)
        val_bytes = tile("val_bytes", T, U8)
        query_raw = tile("query_raw", PACK * Q, F32)
        gout_raw = tile("gout_raw", PACK * Q, F32)
        prior = tile("prior", T, F32)
        result = tile("result", T, F32)
        placed = tile("placed", T, F32)
        s = tile("s", 1, F32)
        row_factor = tile("row_factor", 1, F32)

        def load_scale_rows(scale_tile, rows):
            for n in range(P // QUADRANT):
                nc.sync.dma_start(
                    out=scale_tile[QUADRANT * n:QUADRANT * n + SCALE_ROWS, :].bitcast(I32),
                    in_=rows[0, SCALE_ROWS * n:SCALE_ROWS * (n + 1), :].bitcast(I32))

        def load_rows(raw, src):
            nc.sync.dma_start(out=raw[:], in_=src.rearrange("(p t) q -> p (t q)", t=PACK))

        nc.vector.memset(key_bytes[:].bitcast(I32), 0)
        nc.vector.memset(val_bytes[:].bitcast(I32), 0)
        nc.vector.memset(placed[:], 0.0)

        nc.sync.dma_start(offsets[:], offs)
        nc.sync.dma_start(out=key_words[:].bitcast(I32), in_=keys_words[0].bitcast(I32))
        load_scale_rows(key_bytes, keys_scales)
        load_rows(query_raw, query)
        nc.sync.dma_start(out=val_words[:].bitcast(I32), in_=vals_words[0].bitcast(I32))
        load_rows(gout_raw, gout)
        load_scale_rows(val_bytes, vals_scales)
        nc.sync.dma_start(out=row_factor[:], in_=gq1)
        nc.sync.dma_start(out=prior[:], in_=lprior)
        nc.sync.dma_start(out=s[:], in_=strict)
        nc.sync.dma_start(out=result[:], in_=base)

        def round_and_interleave(name, raw):
            grouped = tile(name, PACK * Q, BF16)
            nc.scalar.activation(grouped[:].rearrange("p (q t) -> p q t", t=PACK),
                                 raw[:].rearrange("p (t q) -> p q t", t=PACK), ACT.Copy)
            return grouped

        def quantise(name, grouped):
            codes = tile(name + "_codes", Q, U32)
            scales = tile(name + "_scales", Q, U8)
            nc.vector.quantize_mx(out=codes[:].bitcast(FP8X4), scales=scales[:], in_=grouped[:])
            return codes, scales

        def gather(name, window, dtype, reuse=None):
            picked = tile(name, I, dtype, reuse=reuse)
            nc.vector.tensor_copy(picked[:], window[:].indirect(offsets[:]))
            return picked

        def product(name, rows_mx, words, scale_bytes):
            codes, scales = rows_mx
            acc = ps.tile([P, I], F32, name=name)
            nc.tensor.matmul_mx(out=acc[:], lhsT=codes[:].bitcast(FP8X4), lhsT_scale=scales[:],
                                rhs=words[:].bitcast(FP4X4), rhs_scale=scale_bytes[:], start=True, stop=True)
            return acc

        query_bf = round_and_interleave("query_bf", query_raw)
        gout_bf = round_and_interleave("gout_bf", gout_raw)

        picked_key_words = gather("picked_key_words", key_words, U16)
        picked_key_bytes = gather("picked_key_bytes", key_bytes, U8)
        query_mx = quantise("query", query_bf)
        a = product("a", query_mx, picked_key_words, picked_key_bytes)
        picked_val_words = gather("picked_val_words", val_words, U16, reuse="query_raw")

        neg_a = tile("neg_a", I, F32)
        neg_max = tile("neg_max", 1, F32)
        nc.vector.tensor_scalar(out=neg_a[:], in0=a[:], scalar1=-1.0, scalar2=None, op0=ALU.mult, op1=ALU.min,
                                accum_out=neg_max[:])
        p = tile("p", I, F32)
        z = tile("z", 1, F32)
        nc.scalar.activation(p[:], neg_a[:], ACT.Exp, bias=neg_max[:], scale=-1.0, accum_out=z[:])

        gout_mx = quantise("gout", gout_bf)
        picked_val_bytes = gather("picked_val_bytes", val_bytes, U8)
        c0 = product("c0", gout_mx, picked_val_words, picked_val_bytes)

        gain = tile("gain", 1, F32)
        neg_gain = tile("neg_gain", 1, F32)
        nc.scalar.activation(gain[:], row_factor[:], ACT.Copy, scale=PENALTY)
        nc.scalar.activation(neg_gain[:], row_factor[:], ACT.Copy, scale=-PENALTY)
        inv_z = tile("inv_z", 1, F32, reuse="row_factor")
        nc.vector.reciprocal(inv_z[:], z[:])

        halves = (slice(0, I // 2), slice(I // 2, I))
        gap = tile("gap", I, F32, reuse="gout_bf")
        for h in halves:
            listed = offsets[:, h.start // LIST_ROWS:h.stop // LIST_ROWS]
            nc.vector.tensor_tensor(gap[:, h], prior[:].indirect(listed), neg_a[:, h], ALU.add)

        w = tile("w", I, F32)
        w_sq = tile("w_sq", I, F32)
        w_gain = tile("w_gain", I, F32)
        w_neg_gain = tile("w_neg_gain", I, F32)
        nc.scalar.activation(w[:], p[:], ACT.Copy, scale=inv_z[:])
        nc.scalar.activation(w_sq[:], p[:], ACT.Square, scale=inv_z[:])
        nc.scalar.activation(w_gain[:], w[:], ACT.Copy, scale=gain[:])
        nc.scalar.activation(w_neg_gain[:], w[:], ACT.Copy, scale=neg_gain[:])

        u = tile("u", I, F32)
        for h in halves:
            nc.vector.scalar_tensor_tensor(u[:, h], gap[:, h], s[:], c0[:, h], ALU.mult, ALU.add)
        wu = tile("wu", I, F32)
        u_mean = tile("u_mean", 1, F32)
        nc.vector.scalar_tensor_tensor(wu[:], u[:], inv_z[:], p[:], ALU.mult, ALU.mult, accum_out=u_mean[:])
        u_mean_s = tile("u_mean_s", 1, F32)
        nc.scalar.activation(u_mean_s[:], u_mean[:], ACT.Identity, bias=s[:])
        d = tile("d", I, F32)
        nc.vector.scalar_tensor_tensor(d[:], u[:], u_mean[:], w[:], ALU.subtract, ALU.mult)
        wd = tile("wd", I, F32)
        sum_wd = tile("sum_wd", 1, F32)
        nc.vector.scalar_tensor_tensor(wd[:], u[:], u_mean[:], w_sq[:], ALU.subtract, ALU.mult, accum_out=sum_wd[:])
        dd = tile("dd", I, F32)
        sum_dd = tile("sum_dd", 1, F32)
        nc.scalar.activation(dd[:], d[:], ACT.Square, accum_out=sum_dd[:])
        second = tile("second", I, F32)
        nc.scalar.activation(second[:], w_neg_gain[:], ACT.Copy, scale=sum_dd[:])
        y = tile("y", I, F32)
        first = tile("first", I, F32)
        for h in halves:
            nc.vector.scalar_tensor_tensor(y[:, h], u[:, h], u_mean_s[:], w_gain[:, h], ALU.subtract, ALU.mult)
        for h in halves:
            nc.vector.scalar_tensor_tensor(first[:, h], d[:, h], sum_wd[:], y[:, h], ALU.subtract, ALU.mult)

        nc.vector.tensor_tensor(placed[:].indirect(offsets[:]), first[:], second[:], ALU.add)

        start = 0
        for width in STORE_WIDTHS:
            cols = slice(start, start + width)
            nc.vector.tensor_tensor(result[:, cols], result[:, cols], placed[:, cols], ALU.add)
            nc.sync.dma_start(out=out[:, cols], in_=result[:, cols])
            start += width
